import numpy as np
import ml_dtypes


def mxq(x, axis, fmt="e4m3"):
    dtype, down = {"e4m3": (ml_dtypes.float8_e4m3fn, 7), "e5m2": (ml_dtypes.float8_e5m2, 14)}[fmt]
    v = np.moveaxis(np.asarray(x, np.float32).astype(ml_dtypes.bfloat16).astype(np.float64), axis, -1)
    blocks = v.reshape(v.shape[:-1] + (-1, 32))
    amax = np.abs(blocks).max(-1, keepdims=True)
    byte = np.maximum(np.where(amax > 0, np.frexp(amax)[1] - 1 + 127, 0) - down, 1)
    scale = np.exp2(byte - 127.0)
    codes = (blocks / scale).astype(np.float32).astype(dtype).astype(np.float64)
    return np.moveaxis((codes * scale).reshape(v.shape), -1, axis)


WIDE = False


def mx_kscale(k):
    if not WIDE:
        return np.ones(k)
    levels = np.array([10, -10, 5, -5, 0])
    if k % 512:
        return np.exp2(np.random.permutation(np.resize(levels, k // 32))).repeat(32)
    a = np.empty((k // 512, 16))
    for p in range(k // 512):
        a[p, :8] = np.random.permutation(np.resize(levels, 8))
        for g in range(8):
            far = levels[np.abs(levels - a[p, g]) >= 10]
            a[p, g + 8] = far[np.random.randint(len(far))]
    return np.exp2(a.ravel()).repeat(32)


def f64(x):
    return np.asarray(x).astype(np.float64)


def striped(idx):
    return np.tile(np.asarray(idx).reshape(-1, 16).T, (8, 1)).astype(np.uint16)


def unstriped(offs):
    return offs[:16].T.reshape(-1).astype(np.int64)


E2M1 = np.array([0.0, 0.5, 1.0, 1.5, 2.0, 3.0, 4.0, 6.0, -0.0, -0.5, -1.0, -1.5, -2.0, -3.0, -4.0, -6.0])


def pack_weight(w, fmt):
    k, n = w.shape
    w = f64(np.asarray(w, np.float32).astype(ml_dtypes.bfloat16)).reshape(k // 32, 32, n)
    amax = np.abs(w).max(1)
    if fmt == "e4m3":
        byte = np.frexp(amax)[1] - 1 + 127 - 7
    else:
        mant, ex = np.frexp(amax / 6.0)
        byte = np.where(mant > 0.5, ex, ex - 1) + 127
    byte = np.clip(np.where(amax > 0, byte, 1), 1, 254)
    scaled = (w * np.exp2(127.0 - byte)[:, None, :]).reshape(k, n).astype(np.float32)
    by_word = np.ascontiguousarray(scaled.reshape(k // 512, 128, 4, n).transpose(0, 1, 3, 2))
    if fmt == "e4m3":
        words = by_word.astype(ml_dtypes.float8_e4m3fn).view(np.uint8)
    else:
        c = by_word.astype(ml_dtypes.float4_e2m1fn).view(np.uint8) & 0xF
        words = (c[..., 0::2] | (c[..., 1::2] << 4)).reshape(k // 512, 128, 2 * n)
    return np.ascontiguousarray(words), np.ascontiguousarray(byte.astype(np.uint8).reshape(k // 512, 16, n))


def unpack_weight(words, scales, fmt):
    g, _, n = scales.shape
    words = np.ascontiguousarray(words).reshape(g, 128, n, -1)
    if fmt == "e4m3":
        vals = words.view(ml_dtypes.float8_e4m3fn).astype(np.float64)
    else:
        nib = np.empty((g, 128, n, 4), np.uint8)
        nib[..., 0::2] = words & 0xF
        nib[..., 1::2] = words >> 4
        vals = E2M1[nib]
    vals = vals * np.repeat(np.exp2(scales.astype(np.float64) - 127.0), 8, axis=1)[..., None]
    return vals.transpose(0, 1, 3, 2).reshape(g * 512, n)


def sigmoid(v):
    return 1.0 / (1.0 + np.exp(-v))


D, E, T, I, Q, G, U = 512, 512, 1024, 256, 512, 16, 1024


def setup_inputs():
    n = np.random.standard_normal
    idx = np.random.permutation(T)[:I]
    idx4 = np.random.permutation(U)[:I]
    fd = mx_kscale(D)
    fe = mx_kscale(E)
    fq = mx_kscale(Q)
    keysp = pack_weight(n((D, T)) / fd[:, None], "e2m1")
    valsp = pack_weight(n((E, T)) / fe[:, None], "e2m1")
    return {
        "query": (n((D, Q)) * 0.8 / np.sqrt(D) * fd[:, None]).astype(np.float32),
        "keys_words": keysp[0],
        "keys_scales": keysp[1],
        "th": (np.random.uniform(-0.5, 0.5, (Q, 1))).astype(np.float32),
        "sharp": (np.random.uniform(1.0, 3.0, (Q, 1))).astype(np.float32),
        "gout": (n((E, Q)) * 1 / np.sqrt(E) * fe[:, None]).astype(np.float32),
        "vals_words": valsp[0],
        "vals_scales": valsp[1],
        "qs": (np.random.uniform(6.25, 25.0, (Q, 1)) * fq[:, None]).astype(np.float32),
        "qrows": (n((Q, D)) / fq[:, None]).astype(np.float32),
        "old": (n((D, U)) * 4.0).astype(np.float32),
        "fade": (np.random.uniform(0.5, 1.0, (1, U))).astype(np.float32),
        "offs": striped(idx),
        "offs4": striped(idx4),
    }


def reference(query, keys_words, keys_scales, th, sharp, gout, vals_words, vals_scales, qs, qrows, old, fade, offs, offs4):
    idx = unstriped(offs)
    idx4 = unstriped(offs4)
    keysu = unpack_weight(keys_words, keys_scales, "e2m1")
    valsu = unpack_weight(vals_words, vals_scales, "e2m1")
    queryq = mxq(f64(query), 0, "e4m3")
    keysidxg = keysu[:, idx]
    a = queryq.T @ keysidxg
    s = a.reshape(Q, G, I // G).mean(axis=2) * f64(sharp)
    p = np.exp(s - np.max(s, axis=1, keepdims=True))
    z = np.sum(p, axis=1, keepdims=True)
    r = p / z
    rr = np.repeat(r, I // G, axis=1)
    goutq = mxq(f64(gout), 0, "e4m3")
    valsidxg = valsu[:, idx]
    c0 = goutq.T @ valsidxg
    drr = c0 * sigmoid(a - f64(th))
    dr = drr.reshape(Q, G, I // G).sum(axis=2)
    dz = np.sum(dr * p / np.square(z) * (-1.0), axis=1, keepdims=True)
    dp = dr / z + dz
    ds = dp * p
    e1 = ds * f64(sharp) / 16.0
    r1 = np.repeat(e1, I // G, axis=1)
    da = c0 * rr * sigmoid(a - f64(th)) * (1.0 - sigmoid(a - f64(th))) + r1
    gs = da * f64(qs)
    qrowsq = mxq(f64(qrows), 0, "e4m3")
    gsq = mxq(gs, 0, "e4m3")
    gk = qrowsq.T @ gsq
    gf = np.zeros((D, U))
    gf[:, idx4] = gk
    y = f64(old) * f64(fade) + gf
    return y

@@ -1,0 +1,322 @@
+from contextlib import ExitStack
+
+import concourse.mybir as mybir
+from concourse.masks import make_identity
+
+D, E, T, I, Q, G, U = 512, 512, 1024, 256, 512, 16, 1024
+FLOPS = 2 * Q * I * D + 2 * Q * I * E + 2 * D * I * Q
+
+F32 = mybir.dt.float32
+BF16 = mybir.dt.bfloat16
+I32 = mybir.dt.int32
+U32 = mybir.dt.uint32
+U16 = mybir.dt.uint16
+U8 = mybir.dt.uint8
+FP8X4 = mybir.dt.float8_e4m3fn_x4
+FP4X4 = mybir.dt.float4_e2m1fn_x4
+ALU = mybir.AluOpType
+ACT = mybir.ActivationFunctionType
+AX = mybir.AxisListType
+
+P = 128
+PACK = 4
+PAGE = I // G
+HALF = I // 2
+BANK = 512
+
+
+def tile_attend_bpagetimessigmoid_k_kernel(
+    tc, query, keys_words, keys_scales, th, sharp, gout, vals_words, vals_scales, qs, qrows, old, fade, offs, offs4, out
+):
+    nc = tc.nc
+    with ExitStack() as ctx:
+        sb = ctx.enter_context(tc.tile_pool(name="sb", bufs=1))
+        ps = ctx.enter_context(tc.psum_pool(name="ps", bufs=1))
+
+        def bank(n, name):
+            return ps.tile([P, BANK], F32, name=name, tag="bank%d" % n)
+
+        slots = sb.tile([P, I // 16], U16, name="slots")
+        places = sb.tile([P, I // 16], U16, name="places")
+        k_scales = sb.tile([P, T], U8, name="k_scales")
+        v_scales = sb.tile([P, T], U8, name="v_scales")
+        k_words = sb.tile([P, T], U16, name="k_words")
+        v_words = sb.tile([P, T], U16, name="v_words")
+
+        def load_scales(tile, scales):
+            for quad in range(4):
+                nc.sync.dma_start(
+                    out=tile[32 * quad : 32 * quad + 32, :].bitcast(I32),
+                    in_=scales[:, 4 * quad : 4 * quad + 4, :].bitcast(I32).to_broadcast([8, 4, T // 4]),
+                )
+
+        def load_rows(name, rows):
+            raw = sb.tile([P, PACK, 512], F32, name=name)
+            nc.sync.dma_start(out=raw[:], in_=rows.rearrange("(p j) w -> p j w", j=PACK))
+            return raw
+
+        def load_halves(name, rows):
+            halves = []
+            for h in range(2):
+                raw = sb.tile([P, PACK, Q // 2], F32, name="%s%d" % (name, h), tag="%s%d" % (name, h))
+                nc.sync.dma_start(out=raw[:], in_=rows[:, h * Q // 2 : (h + 1) * Q // 2].rearrange("(p j) w -> p j w", j=PACK))
+                halves.append(raw)
+            return halves
+
+        def load_column(queue, name, vec):
+            col = sb.tile([P, PACK], F32, name=name)
+            queue.dma_start(out=col[:], in_=vec.rearrange("(p r) o -> p (r o)", r=PACK))
+            return col
+
+        nc.sync.dma_start(slots[:], offs)
+        nc.sync.dma_start(out=k_words[:].bitcast(I32), in_=keys_words[0].bitcast(I32))
+        load_scales(k_scales, keys_scales)
+        query_raw = load_halves("query_raw", query)
+        nc.sync.dma_start(out=v_words[:].bitcast(I32), in_=vals_words[0].bitcast(I32))
+        load_scales(v_scales, vals_scales)
+        th_sb = load_column(nc.sync, "th_sb", th)
+        gout_raw = load_halves("gout_raw", gout)
+        sharp_sb = load_column(nc.sync, "sharp_sb", sharp)
+        qrows_raw = load_rows("qrows_raw", qrows)
+        qs_sb = load_column(nc.sync, "qs_sb", qs)
+        fade_rows = sb.tile([P, P], F32, name="fade_rows")
+        nc.gpsimd.memset(fade_rows[:], 0.0)
+        nc.sync.dma_start(out=fade_rows[0:8, :], in_=fade.rearrange("o (k p) -> (o k) p", p=P))
+        old_sb = []
+        for h in range(2):
+            part = sb.tile([P, 4, BANK], F32, name="old%d" % h)
+            nc.sync.dma_start(out=part[:], in_=old[:, h * BANK : (h + 1) * BANK].rearrange("(m p) u -> p m u", p=P))
+            old_sb.append(part)
+        nc.sync.dma_start(places[:], offs4)
+
+        ident = sb.tile([P, P], F32, name="ident")
+        make_identity(nc, ident[:])
+
+        half_th = sb.tile([P, PACK], F32, name="half_th")
+        sharp16 = sb.tile([P, PACK], F32, name="sharp16")
+        factors = sb.tile([P, 2, PACK], F32, name="factors")
+        nc.vector.tensor_scalar(half_th[:], th_sb[:], -0.5, 0.0, ALU.mult, ALU.add)
+        nc.vector.tensor_scalar(sharp16[:], sharp_sb[:], 1.0 / 16.0, 0.0, ALU.mult, ALU.add)
+        nc.vector.tensor_scalar(factors[:, 0, :], qs_sb[:], -0.25, 0.0, ALU.mult, ALU.add)
+        nc.vector.tensor_scalar(factors[:, 1, :], sharp_sb[:], 0.125, 0.0, ALU.mult, ALU.add)
+
+        windows = []
+        for m in range(2):
+            window = sb.tile([P, U], F32, name="window%d" % m)
+            nc.vector.memset(window[:], 0.0)
+            windows.append(window)
+
+        def gather(name, words, scales):
+            gw = sb.tile([P, I], U16, name=name + "_w", align_bytes=64)
+            picked = sb.tile([P, I], U8, name=name + "_s", align_bytes=64)
+            nc.vector.tensor_copy(gw[:], words[:].indirect(slots[:]))
+            nc.vector.tensor_copy(picked[:], scales[:].indirect(slots[:]))
+            return gw, picked
+
+        def quantize(name, grouped, width):
+            codes = sb.tile([P, width], U32, name=name + "_codes", align_bytes=64)
+            plane = sb.tile([P, width], U8, name=name + "_plane", align_bytes=64)
+            nc.vector.quantize_mx(out=codes[:].bitcast(FP8X4), scales=plane[:], in_=grouped)
+            return codes, plane
+
+        def deal(name, halves):
+            grouped = sb.tile([P, PACK, P, PACK], BF16, name=name + "_bf", align_bytes=64)
+            src = [raw[:].rearrange("p j (s r) -> p s j r", r=PACK) for raw in halves]
+            dst = grouped[:].rearrange("p r s j -> p s j r")
+            nc.scalar.copy(dst[:, 0 : P // 2], src[0])
+            nc.vector.tensor_copy(dst[:, P // 2 : P, :, 0:2], src[1][:, :, :, 0:2])
+            nc.scalar.copy(dst[:, P // 2 : P, :, 2:4], src[1][:, :, :, 2:4])
+            return [grouped[:, 2 * pair : 2 * pair + 2].rearrange("p r s j -> p (r s j)") for pair in range(2)]
+
+        kg_words, kg_scales = gather("kg", k_words, k_scales)
+        q_grouped = deal("query", query_raw)
+        q_quant = [quantize("query%d" % pair, q_grouped[pair], 2 * P) for pair in range(2)]
+
+        a_banks = [bank(0, "a0"), bank(1, "a1")]
+        for r in range(PACK):
+            codes, plane = q_quant[r // 2]
+            cols = slice((r % 2) * P, (r % 2 + 1) * P)
+            nc.tensor.matmul_mx(
+                out=a_banks[r // 2][:, (r % 2) * I : (r % 2 + 1) * I],
+                lhsT=codes[:, cols].bitcast(FP8X4), lhsT_scale=plane[:, cols],
+                rhs=kg_words[:].bitcast(FP4X4), rhs_scale=kg_scales[:],
+                start=True, stop=True,
+            )
+
+        vg_words, vg_scales = gather("vg", v_words, v_scales)
+        page_sum = sb.tile([P, PACK, G], F32, name="page_sum")
+        for pair in range(2):
+            nc.vector.tensor_reduce(
+                out=page_sum[:, 2 * pair : 2 * pair + 2, :].rearrange("p r g -> p (r g)"),
+                in_=a_banks[pair][:].rearrange("p (x j) -> p x j", j=PAGE), axis=AX.X, op=ALU.add,
+            )
+        g_grouped = deal("gout", gout_raw)
+        tanh_sb = sb.tile([P, 2, PACK, HALF], F32, name="tanh_sb", tag="gout_raw1")
+        for r in range(PACK):
+            nc.scalar.activation(
+                out=tanh_sb[:, :, r, :],
+                in_=a_banks[r // 2][:, (r % 2) * I : (r % 2 + 1) * I].rearrange("p (h i) -> p h i", h=2),
+                func=ACT.Tanh, bias=half_th[:, r : r + 1], scale=0.5,
+            )
+        g_quant = [quantize("gout%d" % pair, g_grouped[pair], 2 * P) for pair in range(2)]
+        score = sb.tile([P, PACK, G], F32, name="score")
+        nc.vector.tensor_tensor(score[:], page_sum[:], sharp16[:].unsqueeze(2).to_broadcast([P, PACK, G]), ALU.mult)
+        neg_max = sb.tile([P, PACK], F32, name="neg_max")
+        nc.vector.tensor_reduce(out=neg_max[:], in_=score[:], axis=AX.X, op=ALU.max, negate=True)
+        c_banks = [bank(2, "c0"), bank(3, "c1")]
+        for h in range(2):
+            for r in range(PACK):
+                codes, plane = g_quant[r // 2]
+                cols = slice((r % 2) * P, (r % 2 + 1) * P)
+                half = slice(h * HALF, (h + 1) * HALF)
+                nc.tensor.matmul_mx(
+                    out=c_banks[h][:, r * HALF : (r + 1) * HALF],
+                    lhsT=codes[:, cols].bitcast(FP8X4), lhsT_scale=plane[:, cols],
+                    rhs=vg_words[:, half].bitcast(FP4X4), rhs_scale=vg_scales[:, half],
+                    start=True, stop=True,
+                )
+
+        expo = sb.tile([P, PACK, G], F32, name="expo")
+        z = sb.tile([P, PACK], F32, name="z")
+        for r in range(PACK):
+            nc.scalar.activation(out=expo[:, r, :], in_=score[:, r, :], func=ACT.Exp, bias=neg_max[:, r : r + 1], scale=1.0,
+                                 accum_out=z[:, r : r + 1])
+
+        inv_z = sb.tile([P, PACK], F32, name="inv_z")
+        nc.vector.reciprocal(inv_z[:], z[:])
+        coef = sb.tile([P, 2, PACK], F32, name="coef")
+        nc.vector.tensor_tensor(coef[:], factors[:], inv_z[:].unsqueeze(1).to_broadcast([P, 2, PACK]), ALU.mult)
+        share = sb.tile([P, 2, G, PACK], F32, name="share")
+        nc.vector.tensor_tensor(
+            share[:],
+            expo[:].rearrange("p r g -> p g r").unsqueeze(1).to_broadcast([P, 2, G, PACK]),
+            coef[:].unsqueeze(2).to_broadcast([P, 2, G, PACK]), ALU.mult,
+        )
+
+        square = sb.tile([P, 2, HALF, PACK], F32, name="square")
+        for h in range(2):
+            nc.scalar.activation(out=square[:, h], in_=tanh_sb[:, h].rearrange("p r i -> p i r"), func=ACT.Square)
+
+        gated = sb.tile([P, 2, PACK, HALF], F32, name="gated")
+        for h in range(2):
+            nc.vector.scalar_tensor_tensor(
+                out=gated[:, h].rearrange("p r i -> p (r i)"), in0=tanh_sb[:, h].rearrange("p r i -> p (r i)"), scalar=1.0,
+                in1=c_banks[h][:], op0=ALU.add, op1=ALU.mult,
+            )
+        page_grad = sb.tile([P, G, PACK], F32, name="page_grad")
+        nc.vector.tensor_reduce(
+            out=page_grad[:].rearrange("p (h g) r -> p h r g", h=2),
+            in_=gated[:].rearrange("p h r (g j) -> p h r g j", j=PAGE), axis=AX.X, op=ALU.add,
+        )
+        weighted = sb.tile([P, G, PACK], F32, name="weighted")
+        nc.vector.tensor_tensor(weighted[:], page_grad[:], share[:, 1], ALU.mult)
+        scaled = sb.tile([P, G, PACK], F32, name="scaled")
+        nc.vector.tensor_tensor(scaled[:], page_grad[:], factors[:, 1, :].unsqueeze(1).to_broadcast([P, G, PACK]), ALU.mult)
+        slope = sb.tile([P, 2, HALF, PACK], F32, name="slope")
+
+        def make_slope(h):
+            nc.vector.scalar_tensor_tensor(
+                out=slope[:, h], in0=square[:, h], scalar=-1.0,
+                in1=c_banks[h][:].rearrange("p (r i) -> p i r", r=PACK), op0=ALU.add, op1=ALU.mult,
+            )
+
+        make_slope(0)
+        mean = sb.tile([P, PACK], F32, name="mean")
+        nc.vector.tensor_reduce(out=mean[:], in_=weighted[:].rearrange("p g r -> p r g"), axis=AX.X, op=ALU.add)
+        make_slope(1)
+        centred = sb.tile([P, G, PACK], F32, name="centred")
+        nc.vector.tensor_tensor(centred[:], scaled[:], mean[:].unsqueeze(1).to_broadcast([P, G, PACK]), ALU.subtract)
+
+        qrows_bf = sb.tile([P, D, PACK], BF16, name="qrows_bf", align_bytes=64)
+        nc.scalar.copy(
+            qrows_bf[:].rearrange("p (c i) j -> p c j i", i=4), qrows_raw[:].rearrange("p j (c i) -> p c j i", i=4)
+        )
+
+        total = [sb.tile([P, G // 2, PAGE, PACK], F32, name="total%d" % h) for h in range(2)]
+        gs_bf = [sb.tile([P, G // 2, PAGE, PACK], BF16, name="gs_bf%d" % h, align_bytes=64) for h in range(2)]
+        pages = [slice(0, G // 2), slice(G // 2, G)]
+        wide = [P, G // 2, PAGE, PACK]
+
+        def make_total(h):
+            nc.vector.tensor_tensor(
+                total[h][:], slope[:, h].rearrange("p (g j) r -> p g j r", j=PAGE),
+                centred[:, pages[h], :].unsqueeze(2).to_broadcast(wide), ALU.subtract,
+            )
+
+        def make_gs(h):
+            nc.vector.tensor_tensor(gs_bf[h][:], total[h][:], share[:, 0, pages[h], :].unsqueeze(2).to_broadcast(wide), ALU.mult)
+
+        def quantize_gs(h):
+            return quantize("gs%d" % h, gs_bf[h][:].rearrange("p g j r -> p (g j r)"), HALF)
+
+        make_total(0)
+        r_codes, r_plane = quantize("qrows", qrows_bf[:].rearrange("p d j -> p (d j)"), D)
+        make_gs(0)
+        make_total(1)
+        gs_quant = [quantize_gs(0)]
+        make_gs(1)
+        gs_quant.append(quantize_gs(1))
+
+        fade_bank = bank(4, "fade_bank")
+        nc.tensor.transpose(fade_bank[:, 0:P], fade_rows[:], ident[:])
+        fade_col = sb.tile([P, 8], F32, name="fade_col")
+        nc.scalar.copy(fade_col[:], fade_bank[:, 0:8])
+        faded = []
+
+        def fade_block(k):
+            stage = bank(4 + 2 * (k // 4) + (k + 1) % 2, "stage%d" % k)
+            for m in range(4):
+                nc.tensor.transpose(stage[:, m * P : (m + 1) * P], old_sb[k // 4][:, m, (k % 4) * P : (k % 4 + 1) * P], ident[:])
+            turned = sb.tile([P, D], F32, name="faded%d" % k)
+            nc.scalar.activation(out=turned[:], in_=stage[:], func=ACT.Copy, scale=fade_col[:, k : k + 1])
+            faded.append(turned)
+
+        for k in range(4):
+            fade_block(k)
+
+        gk_banks = [bank(4, "gk0"), bank(5, "gk1")]
+        for h in range(2):
+            codes, plane = gs_quant[h]
+            for m in range(4):
+                cols = slice(m * P, (m + 1) * P)
+                nc.tensor.matmul_mx(
+                    out=gk_banks[h][:, m * HALF : (m + 1) * HALF],
+                    lhsT=r_codes[:, cols].bitcast(FP8X4), lhsT_scale=r_plane[:, cols],
+                    rhs=codes[:].bitcast(FP8X4), rhs_scale=plane[:], start=True, stop=True,
+                )
+        gk_sb = [sb.tile([P, 2, I], F32, name="gk_sb%d" % pair) for pair in range(2)]
+        for h in range(2):
+            for pair in range(2):
+                nc.scalar.copy(
+                    gk_sb[pair][:, :, h * HALF : (h + 1) * HALF],
+                    gk_banks[h][:, 2 * pair * HALF : (2 * pair + 2) * HALF].rearrange("p (m i) -> p m i", m=2),
+                )
+
+        for k in range(4, 8):
+            fade_block(k)
+        out_banks = [0, 1, 2, 3, 4, 5, 6, 7]
+
+        def scatter(m):
+            nc.vector.tensor_copy(windows[m % 2][:].indirect(places[:]), gk_sb[m // 2][:, m % 2, :])
+
+        def finish(m):
+            for h in range(2):
+                acc = bank(out_banks[2 * m + h], "acc%d%d" % (m, h))
+                for kk in range(4):
+                    nc.tensor.transpose(acc[:, kk * P : (kk + 1) * P], faded[4 * h + kk][:, m * P : (m + 1) * P], ident[:])
+                res = sb.tile([P, BANK], F32, name="res%d%d" % (m, h))
+                nc.vector.tensor_tensor(res[:], acc[:], windows[m % 2][:, h * BANK : (h + 1) * BANK], ALU.add)
+                nc.sync.dma_start(out=out[m * P : (m + 1) * P, h * BANK : (h + 1) * BANK], in_=res[:])
+
+        for h in range(2):
+            for m in range(2):
+                nc.vector.tensor_copy(
+                    windows[m][:].indirect(places[:, h * HALF // 16 : (h + 1) * HALF // 16]),
+                    gk_sb[0][:, m, h * HALF : (h + 1) * HALF],
+                )
+        finish(0)
+        scatter(2)
+        finish(1)
+        scatter(3)
+        finish(2)
+        finish(3)

@@ -101,7 +101,7 @@ def tile_attend_bpagetimessigmoid_k_kernel(
         nc.vector.tensor_scalar(factors[:, 1, :], sharp_sb[:], 0.125, 0.0, ALU.mult, ALU.add)
 
         windows = []
-        for m in range(2):
+        for m in range(4):
             window = sb.tile([P, U], F32, name="window%d" % m)
             nc.vector.memset(window[:], 0.0)
             windows.append(window)
@@ -204,10 +204,11 @@ def tile_attend_bpagetimessigmoid_k_kernel(
                 in1=c_banks[h][:], op0=ALU.add, op1=ALU.mult,
             )
         page_grad = sb.tile([P, G, PACK], F32, name="page_grad")
-        nc.vector.tensor_reduce(
-            out=page_grad[:].rearrange("p (h g) r -> p h r g", h=2),
-            in_=gated[:].rearrange("p h r (g j) -> p h r g j", j=PAGE), axis=AX.X, op=ALU.add,
-        )
+        for h in range(2):
+            nc.vector.tensor_reduce(
+                out=page_grad[:, h * G // 2 : (h + 1) * G // 2, :].rearrange("p g r -> p r g"),
+                in_=gated[:, h].rearrange("p r (g j) -> p r g j", j=PAGE), axis=AX.X, op=ALU.add,
+            )
         weighted = sb.tile([P, G, PACK], F32, name="weighted")
         nc.vector.tensor_tensor(weighted[:], page_grad[:], share[:, 1], ALU.mult)
         scaled = sb.tile([P, G, PACK], F32, name="scaled")
@@ -220,12 +221,12 @@ def tile_attend_bpagetimessigmoid_k_kernel(
                 in1=c_banks[h][:].rearrange("p (r i) -> p i r", r=PACK), op0=ALU.add, op1=ALU.mult,
             )
 
-        make_slope(0)
         mean = sb.tile([P, PACK], F32, name="mean")
         nc.vector.tensor_reduce(out=mean[:], in_=weighted[:].rearrange("p g r -> p r g"), axis=AX.X, op=ALU.add)
-        make_slope(1)
         centred = sb.tile([P, G, PACK], F32, name="centred")
         nc.vector.tensor_tensor(centred[:], scaled[:], mean[:].unsqueeze(1).to_broadcast([P, G, PACK]), ALU.subtract)
+        make_slope(0)
+        make_slope(1)
 
         qrows_bf = sb.tile([P, D, PACK], BF16, name="qrows_bf", align_bytes=64)
         nc.scalar.copy(
@@ -257,24 +258,24 @@ def tile_attend_bpagetimessigmoid_k_kernel(
         make_gs(1)
         gs_quant.append(quantize_gs(1))
 
-        fade_bank = bank(4, "fade_bank")
+        fade_bank = bank(7, "fade_bank")
         nc.tensor.transpose(fade_bank[:, 0:P], fade_rows[:], ident[:])
         fade_col = sb.tile([P, 8], F32, name="fade_col")
         nc.scalar.copy(fade_col[:], fade_bank[:, 0:8])
         faded = []
 
         def fade_block(k):
-            stage = bank(4 + 2 * (k // 4) + (k + 1) % 2, "stage%d" % k)
+            stage = bank(4 + k % 4, "stage%d" % k)
             for m in range(4):
                 nc.tensor.transpose(stage[:, m * P : (m + 1) * P], old_sb[k // 4][:, m, (k % 4) * P : (k % 4 + 1) * P], ident[:])
             turned = sb.tile([P, D], F32, name="faded%d" % k)
             nc.scalar.activation(out=turned[:], in_=stage[:], func=ACT.Copy, scale=fade_col[:, k : k + 1])
             faded.append(turned)
 
-        for k in range(4):
+        for k in range(6):
             fade_block(k)
 
-        gk_banks = [bank(4, "gk0"), bank(5, "gk1")]
+        gk_banks = [bank(6, "gk0"), bank(7, "gk1")]
         for h in range(2):
             codes, plane = gs_quant[h]
             for m in range(4):
@@ -292,31 +293,35 @@ def tile_attend_bpagetimessigmoid_k_kernel(
                     gk_banks[h][:, 2 * pair * HALF : (2 * pair + 2) * HALF].rearrange("p (m i) -> p m i", m=2),
                 )
 
-        for k in range(4, 8):
+        for k in range(6, 8):
             fade_block(k)
-        out_banks = [0, 1, 2, 3, 4, 5, 6, 7]
+        out_banks = [0, 1, 2, 3, 4, 5, 7, 6]
 
         def scatter(m):
-            nc.vector.tensor_copy(windows[m % 2][:].indirect(places[:]), gk_sb[m // 2][:, m % 2, :])
+            nc.vector.tensor_copy(windows[m][:].indirect(places[:]), gk_sb[m // 2][:, m % 2, :])
 
-        def finish(m):
-            for h in range(2):
-                acc = bank(out_banks[2 * m + h], "acc%d%d" % (m, h))
-                for kk in range(4):
-                    nc.tensor.transpose(acc[:, kk * P : (kk + 1) * P], faded[4 * h + kk][:, m * P : (m + 1) * P], ident[:])
-                res = sb.tile([P, BANK], F32, name="res%d%d" % (m, h))
-                nc.vector.tensor_tensor(res[:], acc[:], windows[m % 2][:, h * BANK : (h + 1) * BANK], ALU.add)
-                nc.sync.dma_start(out=out[m * P : (m + 1) * P, h * BANK : (h + 1) * BANK], in_=res[:])
+        def finish(m, h, on_gpsimd):
+            acc = bank(out_banks[2 * m + h], "acc%d%d" % (m, h))
+            for kk in range(4):
+                nc.tensor.transpose(acc[:, kk * P : (kk + 1) * P], faded[4 * h + kk][:, m * P : (m + 1) * P], ident[:])
+            res = sb.tile([P, BANK], F32, name="res%d%d" % (m, h))
+            placed = windows[m][:, h * BANK : (h + 1) * BANK]
+            if on_gpsimd:
+                kept = sb.tile([P, BANK], F32, name="kept%d%d" % (m, h))
+                nc.scalar.copy(kept[:], acc[:])
+                nc.gpsimd.tensor_tensor(res[:], kept[:], placed, ALU.add)
+            else:
+                nc.vector.tensor_tensor(res[:], acc[:], placed, ALU.add)
+            queue = nc.sync if on_gpsimd else nc.scalar
+            queue.dma_start(out=out[m * P : (m + 1) * P, h * BANK : (h + 1) * BANK], in_=res[:])
 
         for h in range(2):
-            for m in range(2):
-                nc.vector.tensor_copy(
-                    windows[m][:].indirect(places[:, h * HALF // 16 : (h + 1) * HALF // 16]),
-                    gk_sb[0][:, m, h * HALF : (h + 1) * HALF],
-                )
-        finish(0)
+            nc.vector.tensor_copy(
+                windows[0][:].indirect(places[:, h * HALF // 16 : (h + 1) * HALF // 16]),
+                gk_sb[0][:, 0, h * HALF : (h + 1) * HALF],
+            )
+        scatter(1)
         scatter(2)
-        finish(1)
         scatter(3)
-        finish(2)
-        finish(3)
+        for unit in range(8):
+            finish(unit // 2, unit % 2, unit < 5)

from contextlib import ExitStack

import concourse.mybir as mybir
from concourse.masks import make_identity

D, E, T, I, Q, G, U = 512, 512, 1024, 256, 512, 16, 1024
FLOPS = 2 * Q * I * D + 2 * Q * I * E + 2 * D * I * Q

F32 = mybir.dt.float32
BF16 = mybir.dt.bfloat16
I32 = mybir.dt.int32
U32 = mybir.dt.uint32
U16 = mybir.dt.uint16
U8 = mybir.dt.uint8
FP8X4 = mybir.dt.float8_e4m3fn_x4
FP4X4 = mybir.dt.float4_e2m1fn_x4
ALU = mybir.AluOpType
ACT = mybir.ActivationFunctionType
AX = mybir.AxisListType

P = 128
PACK = 4
PAGE = I // G
HALF = I // 2
BANK = 512


def tile_attend_bpagetimessigmoid_k_kernel(
    tc, query, keys_words, keys_scales, th, sharp, gout, vals_words, vals_scales, qs, qrows, old, fade, offs, offs4, out
):
    nc = tc.nc
    with ExitStack() as ctx:
        sb = ctx.enter_context(tc.tile_pool(name="sb", bufs=1))
        ps = ctx.enter_context(tc.psum_pool(name="ps", bufs=1))

        def bank(n, name):
            return ps.tile([P, BANK], F32, name=name, tag="bank%d" % n)

        slots = sb.tile([P, I // 16], U16, name="slots")
        places = sb.tile([P, I // 16], U16, name="places")
        k_scales = sb.tile([P, T], U8, name="k_scales")
        v_scales = sb.tile([P, T], U8, name="v_scales")
        k_words = sb.tile([P, T], U16, name="k_words")
        v_words = sb.tile([P, T], U16, name="v_words")

        def load_scales(tile, scales):
            for quad in range(4):
                nc.sync.dma_start(
                    out=tile[32 * quad : 32 * quad + 32, :].bitcast(I32),
                    in_=scales[:, 4 * quad : 4 * quad + 4, :].bitcast(I32).to_broadcast([8, 4, T // 4]),
                )

        def load_rows(name, rows):
            raw = sb.tile([P, PACK, 512], F32, name=name)
            nc.sync.dma_start(out=raw[:], in_=rows.rearrange("(p j) w -> p j w", j=PACK))
            return raw

        def load_halves(name, rows):
            halves = []
            for h in range(2):
                raw = sb.tile([P, PACK, Q // 2], F32, name="%s%d" % (name, h), tag="%s%d" % (name, h))
                nc.sync.dma_start(out=raw[:], in_=rows[:, h * Q // 2 : (h + 1) * Q // 2].rearrange("(p j) w -> p j w", j=PACK))
                halves.append(raw)
            return halves

        def load_column(queue, name, vec):
            col = sb.tile([P, PACK], F32, name=name)
            queue.dma_start(out=col[:], in_=vec.rearrange("(p r) o -> p (r o)", r=PACK))
            return col

        nc.sync.dma_start(slots[:], offs)
        nc.sync.dma_start(out=k_words[:].bitcast(I32), in_=keys_words[0].bitcast(I32))
        load_scales(k_scales, keys_scales)
        query_raw = load_halves("query_raw", query)
        nc.sync.dma_start(out=v_words[:].bitcast(I32), in_=vals_words[0].bitcast(I32))
        load_scales(v_scales, vals_scales)
        th_sb = load_column(nc.sync, "th_sb", th)
        gout_raw = load_halves("gout_raw", gout)
        sharp_sb = load_column(nc.sync, "sharp_sb", sharp)
        qrows_raw = load_rows("qrows_raw", qrows)
        qs_sb = load_column(nc.sync, "qs_sb", qs)
        fade_rows = sb.tile([P, P], F32, name="fade_rows")
        nc.gpsimd.memset(fade_rows[:], 0.0)
        nc.sync.dma_start(out=fade_rows[0:8, :], in_=fade.rearrange("o (k p) -> (o k) p", p=P))
        old_sb = []
        for h in range(2):
            part = sb.tile([P, 4, BANK], F32, name="old%d" % h)
            nc.sync.dma_start(out=part[:], in_=old[:, h * BANK : (h + 1) * BANK].rearrange("(m p) u -> p m u", p=P))
            old_sb.append(part)
        nc.sync.dma_start(places[:], offs4)

        ident = sb.tile([P, P], F32, name="ident")
        make_identity(nc, ident[:])

        half_th = sb.tile([P, PACK], F32, name="half_th")
        sharp16 = sb.tile([P, PACK], F32, name="sharp16")
        factors = sb.tile([P, 2, PACK], F32, name="factors")
        nc.vector.tensor_scalar(half_th[:], th_sb[:], -0.5, 0.0, ALU.mult, ALU.add)
        nc.vector.tensor_scalar(sharp16[:], sharp_sb[:], 1.0 / 16.0, 0.0, ALU.mult, ALU.add)
        nc.vector.tensor_scalar(factors[:, 0, :], qs_sb[:], -0.25, 0.0, ALU.mult, ALU.add)
        nc.vector.tensor_scalar(factors[:, 1, :], sharp_sb[:], 0.125, 0.0, ALU.mult, ALU.add)

        windows = []
        for m in range(4):
            window = sb.tile([P, U], F32, name="window%d" % m)
            nc.vector.memset(window[:], 0.0)
            windows.append(window)

        def gather(name, words, scales):
            gw = sb.tile([P, I], U16, name=name + "_w", align_bytes=64)
            picked = sb.tile([P, I], U8, name=name + "_s", align_bytes=64)
            nc.vector.tensor_copy(gw[:], words[:].indirect(slots[:]))
            nc.vector.tensor_copy(picked[:], scales[:].indirect(slots[:]))
            return gw, picked

        def quantize(name, grouped, width):
            codes = sb.tile([P, width], U32, name=name + "_codes", align_bytes=64)
            plane = sb.tile([P, width], U8, name=name + "_plane", align_bytes=64)
            nc.vector.quantize_mx(out=codes[:].bitcast(FP8X4), scales=plane[:], in_=grouped)
            return codes, plane

        def deal(name, halves):
            grouped = sb.tile([P, PACK, P, PACK], BF16, name=name + "_bf", align_bytes=64)
            src = [raw[:].rearrange("p j (s r) -> p s j r", r=PACK) for raw in halves]
            dst = grouped[:].rearrange("p r s j -> p s j r")
            nc.scalar.copy(dst[:, 0 : P // 2], src[0])
            nc.vector.tensor_copy(dst[:, P // 2 : P, :, 0:2], src[1][:, :, :, 0:2])
            nc.scalar.copy(dst[:, P // 2 : P, :, 2:4], src[1][:, :, :, 2:4])
            return [grouped[:, 2 * pair : 2 * pair + 2].rearrange("p r s j -> p (r s j)") for pair in range(2)]

        kg_words, kg_scales = gather("kg", k_words, k_scales)
        q_grouped = deal("query", query_raw)
        q_quant = [quantize("query%d" % pair, q_grouped[pair], 2 * P) for pair in range(2)]

        a_banks = [bank(0, "a0"), bank(1, "a1")]
        for r in range(PACK):
            codes, plane = q_quant[r // 2]
            cols = slice((r % 2) * P, (r % 2 + 1) * P)
            nc.tensor.matmul_mx(
                out=a_banks[r // 2][:, (r % 2) * I : (r % 2 + 1) * I],
                lhsT=codes[:, cols].bitcast(FP8X4), lhsT_scale=plane[:, cols],
                rhs=kg_words[:].bitcast(FP4X4), rhs_scale=kg_scales[:],
                start=True, stop=True,
            )

        vg_words, vg_scales = gather("vg", v_words, v_scales)
        page_sum = sb.tile([P, PACK, G], F32, name="page_sum")
        for pair in range(2):
            nc.vector.tensor_reduce(
                out=page_sum[:, 2 * pair : 2 * pair + 2, :].rearrange("p r g -> p (r g)"),
                in_=a_banks[pair][:].rearrange("p (x j) -> p x j", j=PAGE), axis=AX.X, op=ALU.add,
            )
        g_grouped = deal("gout", gout_raw)
        tanh_sb = sb.tile([P, 2, PACK, HALF], F32, name="tanh_sb", tag="gout_raw1")
        for r in range(PACK):
            nc.scalar.activation(
                out=tanh_sb[:, :, r, :],
                in_=a_banks[r // 2][:, (r % 2) * I : (r % 2 + 1) * I].rearrange("p (h i) -> p h i", h=2),
                func=ACT.Tanh, bias=half_th[:, r : r + 1], scale=0.5,
            )
        g_quant = [quantize("gout%d" % pair, g_grouped[pair], 2 * P) for pair in range(2)]
        score = sb.tile([P, PACK, G], F32, name="score")
        nc.vector.tensor_tensor(score[:], page_sum[:], sharp16[:].unsqueeze(2).to_broadcast([P, PACK, G]), ALU.mult)
        neg_max = sb.tile([P, PACK], F32, name="neg_max")
        nc.vector.tensor_reduce(out=neg_max[:], in_=score[:], axis=AX.X, op=ALU.max, negate=True)
        c_banks = [bank(2, "c0"), bank(3, "c1")]
        for h in range(2):
            for r in range(PACK):
                codes, plane = g_quant[r // 2]
                cols = slice((r % 2) * P, (r % 2 + 1) * P)
                half = slice(h * HALF, (h + 1) * HALF)
                nc.tensor.matmul_mx(
                    out=c_banks[h][:, r * HALF : (r + 1) * HALF],
                    lhsT=codes[:, cols].bitcast(FP8X4), lhsT_scale=plane[:, cols],
                    rhs=vg_words[:, half].bitcast(FP4X4), rhs_scale=vg_scales[:, half],
                    start=True, stop=True,
                )

        expo = sb.tile([P, PACK, G], F32, name="expo")
        z = sb.tile([P, PACK], F32, name="z")
        for r in range(PACK):
            nc.scalar.activation(out=expo[:, r, :], in_=score[:, r, :], func=ACT.Exp, bias=neg_max[:, r : r + 1], scale=1.0,
                                 accum_out=z[:, r : r + 1])

        inv_z = sb.tile([P, PACK], F32, name="inv_z")
        nc.vector.reciprocal(inv_z[:], z[:])
        coef = sb.tile([P, 2, PACK], F32, name="coef")
        nc.vector.tensor_tensor(coef[:], factors[:], inv_z[:].unsqueeze(1).to_broadcast([P, 2, PACK]), ALU.mult)
        share = sb.tile([P, 2, G, PACK], F32, name="share")
        nc.vector.tensor_tensor(
            share[:],
            expo[:].rearrange("p r g -> p g r").unsqueeze(1).to_broadcast([P, 2, G, PACK]),
            coef[:].unsqueeze(2).to_broadcast([P, 2, G, PACK]), ALU.mult,
        )

        square = sb.tile([P, 2, HALF, PACK], F32, name="square")
        for h in range(2):
            nc.scalar.activation(out=square[:, h], in_=tanh_sb[:, h].rearrange("p r i -> p i r"), func=ACT.Square)

        gated = sb.tile([P, 2, PACK, HALF], F32, name="gated")
        for h in range(2):
            nc.vector.scalar_tensor_tensor(
                out=gated[:, h].rearrange("p r i -> p (r i)"), in0=tanh_sb[:, h].rearrange("p r i -> p (r i)"), scalar=1.0,
                in1=c_banks[h][:], op0=ALU.add, op1=ALU.mult,
            )
        page_grad = sb.tile([P, G, PACK], F32, name="page_grad")
        for h in range(2):
            nc.vector.tensor_reduce(
                out=page_grad[:, h * G // 2 : (h + 1) * G // 2, :].rearrange("p g r -> p r g"),
                in_=gated[:, h].rearrange("p r (g j) -> p r g j", j=PAGE), axis=AX.X, op=ALU.add,
            )
        weighted = sb.tile([P, G, PACK], F32, name="weighted")
        nc.vector.tensor_tensor(weighted[:], page_grad[:], share[:, 1], ALU.mult)
        scaled = sb.tile([P, G, PACK], F32, name="scaled")
        nc.vector.tensor_tensor(scaled[:], page_grad[:], factors[:, 1, :].unsqueeze(1).to_broadcast([P, G, PACK]), ALU.mult)
        slope = sb.tile([P, 2, HALF, PACK], F32, name="slope")

        def make_slope(h):
            nc.vector.scalar_tensor_tensor(
                out=slope[:, h], in0=square[:, h], scalar=-1.0,
                in1=c_banks[h][:].rearrange("p (r i) -> p i r", r=PACK), op0=ALU.add, op1=ALU.mult,
            )

        mean = sb.tile([P, PACK], F32, name="mean")
        nc.vector.tensor_reduce(out=mean[:], in_=weighted[:].rearrange("p g r -> p r g"), axis=AX.X, op=ALU.add)
        centred = sb.tile([P, G, PACK], F32, name="centred")
        nc.vector.tensor_tensor(centred[:], scaled[:], mean[:].unsqueeze(1).to_broadcast([P, G, PACK]), ALU.subtract)
        make_slope(0)
        make_slope(1)

        qrows_bf = sb.tile([P, D, PACK], BF16, name="qrows_bf", align_bytes=64)
        nc.scalar.copy(
            qrows_bf[:].rearrange("p (c i) j -> p c j i", i=4), qrows_raw[:].rearrange("p j (c i) -> p c j i", i=4)
        )

        total = [sb.tile([P, G // 2, PAGE, PACK], F32, name="total%d" % h) for h in range(2)]
        gs_bf = [sb.tile([P, G // 2, PAGE, PACK], BF16, name="gs_bf%d" % h, align_bytes=64) for h in range(2)]
        pages = [slice(0, G // 2), slice(G // 2, G)]
        wide = [P, G // 2, PAGE, PACK]

        def make_total(h):
            nc.vector.tensor_tensor(
                total[h][:], slope[:, h].rearrange("p (g j) r -> p g j r", j=PAGE),
                centred[:, pages[h], :].unsqueeze(2).to_broadcast(wide), ALU.subtract,
            )

        def make_gs(h):
            nc.vector.tensor_tensor(gs_bf[h][:], total[h][:], share[:, 0, pages[h], :].unsqueeze(2).to_broadcast(wide), ALU.mult)

        def quantize_gs(h):
            return quantize("gs%d" % h, gs_bf[h][:].rearrange("p g j r -> p (g j r)"), HALF)

        make_total(0)
        r_codes, r_plane = quantize("qrows", qrows_bf[:].rearrange("p d j -> p (d j)"), D)
        make_gs(0)
        make_total(1)
        gs_quant = [quantize_gs(0)]
        make_gs(1)
        gs_quant.append(quantize_gs(1))

        fade_bank = bank(7, "fade_bank")
        nc.tensor.transpose(fade_bank[:, 0:P], fade_rows[:], ident[:])
        fade_col = sb.tile([P, 8], F32, name="fade_col")
        nc.scalar.copy(fade_col[:], fade_bank[:, 0:8])
        faded = []

        def fade_block(k):
            stage = bank(4 + k % 4, "stage%d" % k)
            for m in range(4):
                nc.tensor.transpose(stage[:, m * P : (m + 1) * P], old_sb[k // 4][:, m, (k % 4) * P : (k % 4 + 1) * P], ident[:])
            turned = sb.tile([P, D], F32, name="faded%d" % k)
            nc.scalar.activation(out=turned[:], in_=stage[:], func=ACT.Copy, scale=fade_col[:, k : k + 1])
            faded.append(turned)

        for k in range(6):
            fade_block(k)

        gk_banks = [bank(6, "gk0"), bank(7, "gk1")]
        for h in range(2):
            codes, plane = gs_quant[h]
            for m in range(4):
                cols = slice(m * P, (m + 1) * P)
                nc.tensor.matmul_mx(
                    out=gk_banks[h][:, m * HALF : (m + 1) * HALF],
                    lhsT=r_codes[:, cols].bitcast(FP8X4), lhsT_scale=r_plane[:, cols],
                    rhs=codes[:].bitcast(FP8X4), rhs_scale=plane[:], start=True, stop=True,
                )
        gk_sb = [sb.tile([P, 2, I], F32, name="gk_sb%d" % pair) for pair in range(2)]
        for h in range(2):
            for pair in range(2):
                nc.scalar.copy(
                    gk_sb[pair][:, :, h * HALF : (h + 1) * HALF],
                    gk_banks[h][:, 2 * pair * HALF : (2 * pair + 2) * HALF].rearrange("p (m i) -> p m i", m=2),
                )

        for k in range(6, 8):
            fade_block(k)
        out_banks = [0, 1, 2, 3, 4, 5, 7, 6]

        def scatter(m):
            nc.vector.tensor_copy(windows[m][:].indirect(places[:]), gk_sb[m // 2][:, m % 2, :])

        def finish(m, h, on_gpsimd):
            acc = bank(out_banks[2 * m + h], "acc%d%d" % (m, h))
            for kk in range(4):
                nc.tensor.transpose(acc[:, kk * P : (kk + 1) * P], faded[4 * h + kk][:, m * P : (m + 1) * P], ident[:])
            res = sb.tile([P, BANK], F32, name="res%d%d" % (m, h))
            placed = windows[m][:, h * BANK : (h + 1) * BANK]
            if on_gpsimd:
                kept = sb.tile([P, BANK], F32, name="kept%d%d" % (m, h))
                nc.scalar.copy(kept[:], acc[:])
                nc.gpsimd.tensor_tensor(res[:], kept[:], placed, ALU.add)
            else:
                nc.vector.tensor_tensor(res[:], acc[:], placed, ALU.add)
            queue = nc.sync if on_gpsimd else nc.scalar
            queue.dma_start(out=out[m * P : (m + 1) * P, h * BANK : (h + 1) * BANK], in_=res[:])

        for h in range(2):
            nc.vector.tensor_copy(
                windows[0][:].indirect(places[:, h * HALF // 16 : (h + 1) * HALF // 16]),
                gk_sb[0][:, 0, h * HALF : (h + 1) * HALF],
            )
        scatter(1)
        scatter(2)
        scatter(3)
        for unit in range(8):
            finish(unit // 2, unit % 2, unit < 5)
